import numpy as np
import ml_dtypes


def mxq(x, axis, fmt="e4m3"):
    dtype, down = {"e4m3": (ml_dtypes.float8_e4m3fn, 7), "e5m2": (ml_dtypes.float8_e5m2, 14)}[fmt]
    v = np.moveaxis(np.asarray(x, np.float32).astype(ml_dtypes.bfloat16).astype(np.float64), axis, -1)
    blocks = v.reshape(v.shape[:-1] + (-1, 32))
    amax = np.abs(blocks).max(-1, keepdims=True)
    byte = np.maximum(np.where(amax > 0, np.frexp(amax)[1] - 1 + 127, 0) - down, 1)
    scale = np.exp2(byte - 127.0)
    codes = (blocks / scale).astype(np.float32).astype(dtype).astype(np.float64)
    return np.moveaxis((codes * scale).reshape(v.shape), -1, axis)


WIDE = False


def mx_kscale(k):
    if not WIDE:
        return np.ones(k)
    levels = np.array([10, -10, 5, -5, 0])
    if k % 512:
        return np.exp2(np.random.permutation(np.resize(levels, k // 32))).repeat(32)
    a = np.empty((k // 512, 16))
    for p in range(k // 512):
        a[p, :8] = np.random.permutation(np.resize(levels, 8))
        for g in range(8):
            far = levels[np.abs(levels - a[p, g]) >= 10]
            a[p, g + 8] = far[np.random.randint(len(far))]
    return np.exp2(a.ravel()).repeat(32)


BF16 = ml_dtypes.bfloat16


def bf(x):
    return np.asarray(x, np.float32).astype(BF16)


def f64(x):
    return np.asarray(x).astype(np.float64)


E2M1 = np.array([0.0, 0.5, 1.0, 1.5, 2.0, 3.0, 4.0, 6.0, -0.0, -0.5, -1.0, -1.5, -2.0, -3.0, -4.0, -6.0])


def pack_weight(w, fmt):
    k, n = w.shape
    w = f64(bf(w)).reshape(k // 32, 32, n)
    amax = np.abs(w).max(1)
    if fmt == "e4m3":
        byte = np.frexp(amax)[1] - 1 + 127 - 7
    else:
        mant, ex = np.frexp(amax / 6.0)
        byte = np.where(mant > 0.5, ex, ex - 1) + 127
    byte = np.clip(np.where(amax > 0, byte, 1), 1, 254)
    scaled = (w * np.exp2(127.0 - byte)[:, None, :]).reshape(k, n).astype(np.float32)
    by_word = np.ascontiguousarray(scaled.reshape(k // 512, 128, 4, n).transpose(0, 1, 3, 2))
    if fmt == "e4m3":
        words = by_word.astype(ml_dtypes.float8_e4m3fn).view(np.uint8)
    else:
        c = by_word.astype(ml_dtypes.float4_e2m1fn).view(np.uint8) & 0xF
        words = c[..., 0::2] | (c[..., 1::2] << 4)
    return np.ascontiguousarray(words), np.ascontiguousarray(byte.astype(np.uint8).reshape(k // 512, 16, n))


def unpack_weight(words, scales, fmt):
    g, p, n, _ = words.shape
    if fmt == "e4m3":
        vals = np.ascontiguousarray(words).view(ml_dtypes.float8_e4m3fn).astype(np.float64)
    else:
        nib = np.empty((g, p, n, 4), np.uint8)
        nib[..., 0::2] = words & 0xF
        nib[..., 1::2] = words >> 4
        vals = E2M1[nib]
    vals = vals * np.repeat(np.exp2(scales.astype(np.float64) - 127.0), 8, axis=1)[..., None]
    return vals.transpose(0, 1, 3, 2).reshape(g * 512, n)
def pack4(w):
    words, scales = pack_weight(w, "e2m1")
    return words.reshape(words.shape[0], 128, -1), scales


def unpack4(words, scales):
    return unpack_weight(words.reshape(words.shape[0], 128, -1, 2), scales, "e2m1")


K, M = 1536, 512

STEP = 1.0 / 3.0
REWARD = 0.3


def setup_inputs():
    s = mx_kscale(K)
    r = 1 / np.sqrt(K) / s[:, None]
    w1_words, w1_scales = pack4(np.random.standard_normal((K, K)) * STEP * r * s)
    w2_words, w2_scales = pack4(np.random.standard_normal((K, K)) * STEP * r * s)
    w3_words, w3_scales = pack4(np.random.standard_normal((K, K)) * r)
    return {"theta": bf(np.random.standard_normal((K, M)) * s[:, None]),
            "w1_words": w1_words, "w1_scales": w1_scales,
            "w2_words": w2_words, "w2_scales": w2_scales,
            "w3_words": w3_words, "w3_scales": w3_scales,
            "b1": bf(np.random.standard_normal(K) * REWARD * s),
            "b2": bf(np.random.standard_normal(K) * REWARD * s),
            "b3": bf(np.random.standard_normal(K) * REWARD)}


def reference(theta, w1_words, w1_scales, w2_words, w2_scales, w3_words, w3_scales, b1, b2, b3):
    w1 = unpack4(w1_words, w1_scales)
    w2 = unpack4(w2_words, w2_scales)
    w3 = unpack4(w3_words, w3_scales)
    v0 = f64(theta)
    a1 = w1.T @ mxq(v0, 0, "e4m3")
    v1 = v0 + (f64(b1)[:, None] - a1)
    a2 = w2.T @ mxq(v1, 0, "e4m3")
    v2 = v1 + (f64(b2)[:, None] - a2)
    a3 = w3.T @ mxq(v2, 0, "e4m3")
    return f64(b3)[:, None] - a3

@@ -1,0 +1,292 @@
+from contextlib import ExitStack
+
+import concourse.mybir as mybir
+from concourse.masks import make_identity
+
+F32 = mybir.dt.float32
+BF16 = mybir.dt.bfloat16
+U32 = mybir.dt.uint32
+I32 = mybir.dt.int32
+U8 = mybir.dt.uint8
+FP8X4 = mybir.dt.float8_e4m3fn_x4
+FP4X4 = mybir.dt.float4_e2m1fn_x4
+ALU = mybir.AluOpType
+ACTF = mybir.ActivationFunctionType
+
+P = 128
+K = 1536
+M = 512
+G = 3
+T = 4
+FLOPS = 3 * 2 * K * K * M
+
+TH_V = [320, 192, 160]
+ON_GPSIMD = {(0, 2), (1, 0), (1, 1), (1, 2)}
+V1_V = [0, 0, 160]
+V2_V = [0, 0, 160]
+
+
+def tile_ensemble_td_updates_t2_kernel(
+    tc, theta, w1_words, w1_scales, w2_words, w2_scales, w3_words, w3_scales, b1, b2, b3, out
+):
+    nc = tc.nc
+    with ExitStack() as ctx:
+        pool = ctx.enter_context(tc.tile_pool(name="keep", bufs=1))
+        psum = ctx.enter_context(tc.psum_pool(name="psum", bufs=1))
+        ctx.enter_context(tc.manual_schedule())
+
+        def sb(name, shape, dtype):
+            return pool.tile(shape, dtype, name=name, tag=name, align_bytes=64)
+
+        def bank(n, name):
+            return psum.tile([P, M], F32, name=name, tag="bank%d" % n)
+
+        dummy = sb("dummy", [P, 1], F32)
+        nc.vector.memset(dummy[:], 0.0)
+        nc.scalar.activation(out=dummy[:], in_=dummy[:], func=ACTF.Identity, scale=1.0)
+
+        th = [sb("th%d" % g, [P, T, M], BF16) for g in range(G)]
+        thg = [sb("thg%d" % g, [P, M, T], BF16) for g in range(G)]
+        q = {}
+        for s in range(3):
+            for g in range(G):
+                q[s, g] = (sb("qc%d%d" % (s, g), [P, M], U32), sb("qs%d%d" % (s, g), [P, M], U8))
+        w1raw = [sb("w1raw%d" % g, [P, G, 1024], U8) for g in range(G)]
+        w2raw = sb("w2raw", [P, G, 3072], U8)
+        w3raw = sb("w3raw", [P, G, 3072], U8)
+        s3 = sb("s3", [P, G, K], U8)
+        pk = [sb("pk%d" % s, [P, K], U8) for s in range(2)]
+        pm = [sb("pm%d" % s, [P, K], U8) for s in range(2)]
+        planes = {(s, k): sb("pl%d%d" % (s, k), [P, K], U8) for s in range(2) for k in range(1, G)}
+        for s in range(2):
+            planes[s, 0] = pm[s]
+        wp = {}
+        for s in range(2):
+            for g in range(G):
+                wp[s, g] = sb("wp%d%d" % (s, g), [P, G, T, 256], U8)
+        bsb = [sb("b%d" % s, [P, G, T], BF16) for s in range(2)]
+        b3rows = sb("b3rows", [P, P], BF16)
+        b3col = sb("b3col", [P, 12], F32)
+        ident = sb("ident", [P, P], BF16)
+        nv1 = [sb("nv1%d" % g, [P, T, M], F32) for g in range(G)]
+        nv1g = [sb("nv1g%d" % g, [P, M, T], BF16) for g in range(G)]
+        v2 = [sb("v2%d" % g, [P, T, M], BF16) for g in range(G)]
+        v2g = [sb("v2g%d" % g, [P, M, T], BF16) for g in range(G)]
+        osb = [sb("o%d" % c, [P, M], F32) for c in range(12)]
+
+        nc.vector.memset(pk[0][:].bitcast(I32), 0)
+        nc.vector.memset(pk[1][:].bitcast(I32), 0)
+        for s in range(2):
+            for k in range(1, G):
+                nc.gpsimd.memset(planes[s, k][:].bitcast(I32), 0)
+        nc.gpsimd.memset(s3[:].rearrange("p g n -> p (g n)").bitcast(I32), 0)
+        nc.gpsimd.memset(b3rows[:], 0.0)
+        make_identity(nc, ident[:])
+
+        def load_theta(g):
+            nc.sync.dma_start(out=th[g][:], in_=theta[512 * g : 512 * (g + 1), :].rearrange("(p j) m -> p j m", j=T))
+
+        def load_w1(g):
+            nc.sync.dma_start(
+                out=w1raw[g][:].bitcast(I32),
+                in_=w1_words.rearrange("k p c -> p k c")[:, :, 1024 * g : 1024 * (g + 1)].bitcast(I32),
+            )
+
+        def load_packed_scales(s, scales):
+            for quad in range(4):
+                row = 32 * quad
+                nc.sync.dma_start(
+                    out=pk[s][row : row + 12, :].bitcast(I32),
+                    in_=scales[:, 4 * quad : 4 * quad + 4, :].bitcast(I32),
+                )
+
+        def load_scales3():
+            for quad in range(4):
+                nc.sync.dma_start(
+                    out=s3[32 * quad : 32 * quad + 4, :, :].bitcast(I32),
+                    in_=w3_scales[:, 4 * quad : 4 * quad + 4, :].rearrange("k r n -> r k n").bitcast(I32),
+                )
+
+        def spread_scales(queue, s, k):
+            for quad in range(4):
+                row = 32 * quad + 4 * k
+                queue.dma_start(
+                    out=planes[s, k][32 * quad : 32 * quad + 4, :].bitcast(I32), in_=pm[s][row : row + 4, :].bitcast(I32)
+                )
+
+        def load_w(raw, words, k):
+            nc.sync.dma_start(out=raw[:, k, :].bitcast(I32), in_=words[k].bitcast(I32))
+
+        load_theta(0)
+        load_packed_scales(0, w1_scales)
+        load_w1(0)
+        load_theta(1)
+        load_w1(1)
+        load_theta(2)
+        load_packed_scales(1, w2_scales)
+        nc.sync.dma_start(out=bsb[0][:], in_=b1.rearrange("(g p t) -> p g t", p=P, t=T))
+        nc.sync.dma_start(out=bsb[1][:], in_=b2.rearrange("(g p t) -> p g t", p=P, t=T))
+        nc.sync.dma_start(out=b3rows[0:12, :], in_=b3.rearrange("(c p) -> c p", p=P))
+        load_w1(2)
+        for k in range(G):
+            load_w(w2raw, w2_words, k)
+
+        def interleave(dst, src, nv):
+            d = dst[:]
+            s = src[:].rearrange("p t m -> p m t")
+            if nv < M:
+                nc.scalar.copy(out=d[:, nv:M, :], in_=s[:, nv:M, :])
+            if nv > 0:
+                nc.vector.tensor_copy(out=d[:, 0:nv, :], in_=s[:, 0:nv, :])
+
+        def quant(s, g, src):
+            codes, scales = q[s, g]
+            nc.vector.quantize_mx(
+                out=codes[:].bitcast(FP8X4), scales=scales[:], in_=src[:].rearrange("p m t -> p (m t)")
+            )
+
+        def perm_codes(s, g, k):
+            raw = w1raw[g][:, k, :] if s == 0 else w2raw[:, k, 1024 * g : 1024 * (g + 1)]
+            eng = nc.gpsimd if (s, g) in ON_GPSIMD else nc.vector
+            eng.tensor_copy(
+                out=wp[s, g][:, k, :, :].rearrange("p t (f b) -> p t f b", b=2),
+                in_=raw.rearrange("p (f t b) -> p t f b", t=T, b=2),
+            )
+
+        acc = {}
+
+        def mm(s, g, t, k):
+            if k == 0:
+                acc[s, g, t] = bank((4 * g + t + 4 * s) % 8, "acc%d_%d_%d" % (s, g, t))
+            if s < 2:
+                lhsT = wp[s, g][:, k, t, :]
+                lsc = planes[s, k][:, 512 * g + P * t : 512 * g + P * (t + 1)]
+            else:
+                c = 4 * g + t
+                lhsT = w3raw[:, k, 256 * c : 256 * (c + 1)]
+                lsc = s3[:, k, P * c : P * (c + 1)]
+            codes, scales = q[s, k]
+            nc.tensor.matmul_mx(
+                out=acc[s, g, t][:],
+                lhsT=lhsT.bitcast(FP4X4),
+                lhsT_scale=lsc,
+                rhs=codes[:].bitcast(FP8X4),
+                rhs_scale=scales[:],
+                start=(k == 0),
+                stop=(k == 2),
+            )
+
+        def st1(g, t):
+            nc.vector.scalar_tensor_tensor(
+                out=nv1[g][:, t, :], in0=acc[0, g, t][:], scalar=bsb[0][:, g, t : t + 1], in1=th[g][:, t, :],
+                op0=ALU.subtract, op1=ALU.subtract,
+            )
+
+        def st2(g, t):
+            nc.vector.scalar_tensor_tensor(
+                out=v2[g][:, t, :], in0=acc[1, g, t][:], scalar=bsb[1][:, g, t : t + 1], in1=nv1[g][:, t, :],
+                op0=ALU.add, op1=ALU.subtract,
+            )
+
+        def st3(g, t, on_vector):
+            c = 4 * g + t
+            if on_vector:
+                nc.vector.tensor_scalar(
+                    out=osb[c][:], in0=acc[2, g, t][:], scalar1=-1.0, scalar2=b3col[:, c : c + 1],
+                    op0=ALU.mult, op1=ALU.add,
+                )
+            else:
+                nc.scalar.activation(
+                    out=osb[c][:], in_=acc[2, g, t][:], func=ACTF.Identity, bias=b3col[:, c : c + 1], scale=-1.0
+                )
+            nc.sync.dma_start(out=out[P * c : P * (c + 1), :], in_=osb[c][:])
+
+        def mmk(s, g, k):
+            for t in range(T):
+                mm(s, g, t, k)
+
+        def mmt(s, g, t):
+            for k in range(G):
+                mm(s, g, t, k)
+
+        def permute_scales(s):
+            nc.vector.tensor_copy(
+                out=pm[s][:].rearrange("p (g t f) -> p g t f", g=G, t=T),
+                in_=pk[s][:].rearrange("p (g f t) -> p g t f", g=G, t=T),
+            )
+
+        interleave(thg[0], th[0], TH_V[0])
+        quant(0, 0, thg[0])
+        permute_scales(0)
+        for k in range(1, G):
+            spread_scales(nc.scalar, 0, k)
+        for k in range(G):
+            if k:
+                interleave(thg[k], th[k], TH_V[k])
+                quant(0, k, thg[k])
+            perm_codes(0, 0, k)
+            mmk(0, 0, k)
+            perm_codes(0, 1, k)
+            mmk(0, 1, k)
+        b3ps = psum.tile([P, P], BF16, name="b3ps", tag="bank0")
+        nc.tensor.transpose(b3ps[:], b3rows[:], ident[:])
+        nc.scalar.copy(out=b3col[:], in_=b3ps[:, 0:12])
+        permute_scales(1)
+        for k in range(1, G):
+            spread_scales(nc.sync, 1, k)
+        load_scales3()
+        for k in range(G):
+            load_w(w3raw, w3_words, k)
+        for k in range(G):
+            perm_codes(0, 2, k)
+        for g in range(G):
+            for k in range(G):
+                perm_codes(1, g, k)
+        for t in range(T):
+            st1(0, t)
+        interleave(nv1g[0], nv1[0], V1_V[0])
+        for t in range(T):
+            mmt(0, 2, t)
+        for t in range(T):
+            st1(1, t)
+        interleave(nv1g[1], nv1[1], V1_V[1])
+        quant(1, 0, nv1g[0])
+        mmk(1, 0, 0)
+        for t in range(T):
+            st1(2, t)
+        mmk(1, 1, 0)
+        interleave(nv1g[2], nv1[2], V1_V[2])
+        quant(1, 1, nv1g[1])
+        mmk(1, 0, 1)
+        mmk(1, 1, 1)
+        quant(1, 2, nv1g[2])
+        mmk(1, 0, 2)
+        mmk(1, 1, 2)
+        for t in range(T):
+            st2(0, t)
+        interleave(v2g[0], v2[0], V2_V[0])
+        for t in range(T):
+            mmt(1, 2, t)
+        for t in range(T):
+            st2(1, t)
+        interleave(v2g[1], v2[1], V2_V[1])
+        quant(2, 0, v2g[0])
+        mmk(2, 0, 0)
+        for t in range(T):
+            st2(2, t)
+        mmk(2, 1, 0)
+        interleave(v2g[2], v2[2], V2_V[2])
+        quant(2, 1, v2g[1])
+        mmk(2, 0, 1)
+        mmk(2, 1, 1)
+        quant(2, 2, v2g[2])
+        mmk(2, 0, 2)
+        for t in range(T):
+            st3(0, t, False)
+        mmk(2, 1, 2)
+        for t in range(T):
+            st3(1, t, t % 2 == 1)
+        for t in range(T):
+            mmt(2, 2, t)
+        for t in range(T):
+            st3(2, t, t % 2 == 1)

@@ -20,10 +20,8 @@ G = 3
 T = 4
 FLOPS = 3 * 2 * K * K * M
 
-TH_V = [320, 192, 160]
-ON_GPSIMD = {(0, 2), (1, 0), (1, 1), (1, 2)}
-V1_V = [0, 0, 160]
-V2_V = [0, 0, 160]
+IV_V = [[320, 160, 96], [0, 0, 160], [0, 0, 160]]
+ON_GPSIMD = [(0, 2, 0), (0, 2, 1), (0, 2, 2), (1, 2, 0), (1, 2, 1), (1, 2, 2)]
 
 
 def tile_ensemble_td_updates_t2_kernel(
@@ -42,9 +40,6 @@ def tile_ensemble_td_updates_t2_kernel(
             return psum.tile([P, M], F32, name=name, tag="bank%d" % n)
 
         dummy = sb("dummy", [P, 1], F32)
-        nc.vector.memset(dummy[:], 0.0)
-        nc.scalar.activation(out=dummy[:], in_=dummy[:], func=ACTF.Identity, scale=1.0)
-
         th = [sb("th%d" % g, [P, T, M], BF16) for g in range(G)]
         thg = [sb("thg%d" % g, [P, M, T], BF16) for g in range(G)]
         q = {}
@@ -63,7 +58,8 @@ def tile_ensemble_td_updates_t2_kernel(
         wp = {}
         for s in range(2):
             for g in range(G):
-                wp[s, g] = sb("wp%d%d" % (s, g), [P, G, T, 256], U8)
+                if g < 2:
+                    wp[s, g] = sb("wp%d%d" % (s, g), [P, G, T, 256], U8)
         bsb = [sb("b%d" % s, [P, G, T], BF16) for s in range(2)]
         b3rows = sb("b3rows", [P, P], BF16)
         b3col = sb("b3col", [P, 12], F32)
@@ -75,6 +71,7 @@ def tile_ensemble_td_updates_t2_kernel(
         osb = [sb("o%d" % c, [P, M], F32) for c in range(12)]
 
         nc.vector.memset(pk[0][:].bitcast(I32), 0)
+        nc.vector.memset(dummy[:], 0.0)
         nc.vector.memset(pk[1][:].bitcast(I32), 0)
         for s in range(2):
             for k in range(1, G):
@@ -92,10 +89,10 @@ def tile_ensemble_td_updates_t2_kernel(
                 in_=w1_words.rearrange("k p c -> p k c")[:, :, 1024 * g : 1024 * (g + 1)].bitcast(I32),
             )
 
-        def load_packed_scales(s, scales):
+        def load_packed_scales(queue, s, scales):
             for quad in range(4):
                 row = 32 * quad
-                nc.sync.dma_start(
+                queue.dma_start(
                     out=pk[s][row : row + 12, :].bitcast(I32),
                     in_=scales[:, 4 * quad : 4 * quad + 4, :].bitcast(I32),
                 )
@@ -118,28 +115,34 @@ def tile_ensemble_td_updates_t2_kernel(
             nc.sync.dma_start(out=raw[:, k, :].bitcast(I32), in_=words[k].bitcast(I32))
 
         load_theta(0)
-        load_packed_scales(0, w1_scales)
+        load_packed_scales(nc.scalar, 0, w1_scales)
+        nc.scalar.activation(out=dummy[:], in_=dummy[:], func=ACTF.Identity, scale=1.0)
         load_w1(0)
         load_theta(1)
         load_w1(1)
         load_theta(2)
-        load_packed_scales(1, w2_scales)
-        nc.sync.dma_start(out=bsb[0][:], in_=b1.rearrange("(g p t) -> p g t", p=P, t=T))
-        nc.sync.dma_start(out=bsb[1][:], in_=b2.rearrange("(g p t) -> p g t", p=P, t=T))
-        nc.sync.dma_start(out=b3rows[0:12, :], in_=b3.rearrange("(c p) -> c p", p=P))
         load_w1(2)
-        for k in range(G):
-            load_w(w2raw, w2_words, k)
 
-        def interleave(dst, src, nv):
-            d = dst[:]
-            s = src[:].rearrange("p t m -> p m t")
-            if nv < M:
-                nc.scalar.copy(out=d[:, nv:M, :], in_=s[:, nv:M, :])
-            if nv > 0:
-                nc.vector.tensor_copy(out=d[:, 0:nv, :], in_=s[:, 0:nv, :])
+        def interleave(engine, dst, src, c0, c1):
+            if c0 < c1:
+                engine(
+                    out=dst[:, c0:c1, :].rearrange("p (c i) t -> p c t i", i=4),
+                    in_=src[:, :, c0:c1].rearrange("p t (c i) -> p c t i", i=4),
+                )
 
-        def quant(s, g, src):
+        def tiles(s, g):
+            return ((th, thg), (nv1, nv1g), (v2, v2g))[s]
+
+        def iv_v(s, g):
+            a, b = tiles(s, g)
+            interleave(nc.vector.tensor_copy, b[g], a[g], 0, IV_V[s][g])
+
+        def iv_s(s, g):
+            a, b = tiles(s, g)
+            interleave(nc.scalar.copy, b[g], a[g], IV_V[s][g], M)
+
+        def quant(s, g):
+            src = tiles(s, g)[1][g]
             codes, scales = q[s, g]
             nc.vector.quantize_mx(
                 out=codes[:].bitcast(FP8X4), scales=scales[:], in_=src[:].rearrange("p m t -> p (m t)")
@@ -147,7 +150,7 @@ def tile_ensemble_td_updates_t2_kernel(
 
         def perm_codes(s, g, k):
             raw = w1raw[g][:, k, :] if s == 0 else w2raw[:, k, 1024 * g : 1024 * (g + 1)]
-            eng = nc.gpsimd if (s, g) in ON_GPSIMD else nc.vector
+            eng = nc.gpsimd if (s, g, k) in ON_GPSIMD else nc.vector
             eng.tensor_copy(
                 out=wp[s, g][:, k, :, :].rearrange("p t (f b) -> p t f b", b=2),
                 in_=raw.rearrange("p (f t b) -> p t f b", t=T, b=2),
@@ -215,78 +218,102 @@ def tile_ensemble_td_updates_t2_kernel(
                 in_=pk[s][:].rearrange("p (g f t) -> p g t f", g=G, t=T),
             )
 
-        interleave(thg[0], th[0], TH_V[0])
-        quant(0, 0, thg[0])
+        def all_k(f, *args):
+            for k in range(G):
+                f(*args, k)
+
+        def all_t(f, *args):
+            for t in range(T):
+                f(*args, t)
+
+        iv_s(0, 0)
+        iv_v(0, 0)
         permute_scales(0)
-        for k in range(1, G):
-            spread_scales(nc.scalar, 0, k)
+        spread_scales(nc.scalar, 0, 1)
+        spread_scales(nc.sync, 0, 2)
+        nc.sync.dma_start(out=bsb[0][:], in_=b1.rearrange("(g p t) -> p g t", p=P, t=T))
+        nc.sync.dma_start(out=bsb[1][:], in_=b2.rearrange("(g p t) -> p g t", p=P, t=T))
+        nc.sync.dma_start(out=b3rows[0:12, :], in_=b3.rearrange("(c p) -> c p", p=P))
+        load_packed_scales(nc.sync, 1, w2_scales)
         for k in range(G):
-            if k:
-                interleave(thg[k], th[k], TH_V[k])
-                quant(0, k, thg[k])
-            perm_codes(0, 0, k)
-            mmk(0, 0, k)
-            perm_codes(0, 1, k)
-            mmk(0, 1, k)
-        b3ps = psum.tile([P, P], BF16, name="b3ps", tag="bank0")
-        nc.tensor.transpose(b3ps[:], b3rows[:], ident[:])
-        nc.scalar.copy(out=b3col[:], in_=b3ps[:, 0:12])
+            load_w(w2raw, w2_words, k)
+        quant(0, 0)
+        perm_codes(0, 0, 0)
+        mmk(0, 0, 0)
+        perm_codes(0, 1, 0)
+        mmk(0, 1, 0)
+        iv_s(0, 1)
+        iv_v(0, 1)
+        perm_codes(0, 0, 1)
+        quant(0, 1)
+        mmk(0, 0, 1)
+        perm_codes(0, 1, 1)
+        mmk(0, 1, 1)
+        iv_s(0, 2)
+        iv_v(0, 2)
+        perm_codes(0, 0, 2)
+        quant(0, 2)
+        mmk(0, 0, 2)
+        perm_codes(0, 1, 2)
+        mmk(0, 1, 2)
         permute_scales(1)
         for k in range(1, G):
             spread_scales(nc.sync, 1, k)
         load_scales3()
         for k in range(G):
             load_w(w3raw, w3_words, k)
-        for k in range(G):
-            perm_codes(0, 2, k)
-        for g in range(G):
-            for k in range(G):
-                perm_codes(1, g, k)
-        for t in range(T):
-            st1(0, t)
-        interleave(nv1g[0], nv1[0], V1_V[0])
-        for t in range(T):
-            mmt(0, 2, t)
-        for t in range(T):
-            st1(1, t)
-        interleave(nv1g[1], nv1[1], V1_V[1])
-        quant(1, 0, nv1g[0])
+        all_t(st1, 0)
+        b3ps = psum.tile([P, P], BF16, name="b3ps", tag="bank0")
+        nc.tensor.transpose(b3ps[:], b3rows[:], ident[:])
+        nc.scalar.copy(out=b3col[:], in_=b3ps[:, 0:12])
+        iv_s(1, 0)
+        wp[0, 2] = pool.tile([P, G, T, 256], U8, name="wp02", tag="pk1", align_bytes=64)
+        all_k(perm_codes, 0, 2)
+        all_t(mmt, 0, 2)
+        all_t(st1, 1)
+        iv_s(1, 1)
+        iv_v(1, 0)
+        perm_codes(1, 0, 0)
+        quant(1, 0)
         mmk(1, 0, 0)
-        for t in range(T):
-            st1(2, t)
+        all_t(st1, 2)
+        iv_s(1, 2)
+        perm_codes(1, 1, 0)
         mmk(1, 1, 0)
-        interleave(nv1g[2], nv1[2], V1_V[2])
-        quant(1, 1, nv1g[1])
+        iv_v(1, 2)
+        perm_codes(1, 0, 1)
+        quant(1, 1)
         mmk(1, 0, 1)
+        perm_codes(1, 1, 1)
         mmk(1, 1, 1)
-        quant(1, 2, nv1g[2])
+        perm_codes(1, 0, 2)
+        perm_codes(1, 1, 2)
+        quant(1, 2)
         mmk(1, 0, 2)
         mmk(1, 1, 2)
-        for t in range(T):
-            st2(0, t)
-        interleave(v2g[0], v2[0], V2_V[0])
-        for t in range(T):
-            mmt(1, 2, t)
-        for t in range(T):
-            st2(1, t)
-        interleave(v2g[1], v2[1], V2_V[1])
-        quant(2, 0, v2g[0])
+        all_t(st2, 0)
+        iv_s(2, 0)
+        wp[1, 2] = pool.tile([P, G, T, 256], U8, name="wp12", tag="nv1g2", align_bytes=64)
+        all_k(perm_codes, 1, 2)
+        all_t(mmt, 1, 2)
+        all_t(st2, 1)
+        iv_s(2, 1)
+        quant(2, 0)
         mmk(2, 0, 0)
-        for t in range(T):
-            st2(2, t)
+        all_t(st2, 2)
+        iv_s(2, 2)
         mmk(2, 1, 0)
-        interleave(v2g[2], v2[2], V2_V[2])
-        quant(2, 1, v2g[1])
+        quant(2, 1)
         mmk(2, 0, 1)
         mmk(2, 1, 1)
-        quant(2, 2, v2g[2])
+        iv_v(2, 2)
+        quant(2, 2)
         mmk(2, 0, 2)
         for t in range(T):
-            st3(0, t, False)
+            st3(0, t, t % 2 == 1)
         mmk(2, 1, 2)
         for t in range(T):
             st3(1, t, t % 2 == 1)
-        for t in range(T):
-            mmt(2, 2, t)
+        all_t(mmt, 2, 2)
         for t in range(T):
             st3(2, t, t % 2 == 1)

@@ -20,8 +20,8 @@ G = 3
 T = 4
 FLOPS = 3 * 2 * K * K * M
 
-IV_V = [[320, 160, 96], [0, 0, 160], [0, 0, 160]]
-ON_GPSIMD = [(0, 2, 0), (0, 2, 1), (0, 2, 2), (1, 2, 0), (1, 2, 1), (1, 2, 2)]
+IV_V = [[224, 0, 96], [0, 0, 0], [0, 0, 336]]
+REUSE = {(0, 2, 1): "thg2", (0, 2, 2): "thg1", (1, 0, 0): "thg0", (1, 0, 1): "nv1g0", (1, 2, 1): "nv1g2", (1, 2, 2): "nv1g1"}
 
 
 def tile_ensemble_td_updates_t2_kernel(
@@ -50,16 +50,12 @@ def tile_ensemble_td_updates_t2_kernel(
         w2raw = sb("w2raw", [P, G, 3072], U8)
         w3raw = sb("w3raw", [P, G, 3072], U8)
         s3 = sb("s3", [P, G, K], U8)
-        pk = [sb("pk%d" % s, [P, K], U8) for s in range(2)]
-        pm = [sb("pm%d" % s, [P, K], U8) for s in range(2)]
-        planes = {(s, k): sb("pl%d%d" % (s, k), [P, K], U8) for s in range(2) for k in range(1, G)}
-        for s in range(2):
-            planes[s, 0] = pm[s]
+        s1 = sb("s1", [P, G, K], U8)
+        sp1 = [sb("sp1%d" % g, [P, T, G, P], U8) for g in range(G)]
+        pk = sb("pk", [P, K], U8)
+        pm = sb("pm", [P, K], U8)
+        planes = [pm] + [sb("pl%d" % k, [P, K], U8) for k in range(1, G)]
         wp = {}
-        for s in range(2):
-            for g in range(G):
-                if g < 2:
-                    wp[s, g] = sb("wp%d%d" % (s, g), [P, G, T, 256], U8)
         bsb = [sb("b%d" % s, [P, G, T], BF16) for s in range(2)]
         b3rows = sb("b3rows", [P, P], BF16)
         b3col = sb("b3col", [P, 12], F32)
@@ -70,15 +66,14 @@ def tile_ensemble_td_updates_t2_kernel(
         v2g = [sb("v2g%d" % g, [P, M, T], BF16) for g in range(G)]
         osb = [sb("o%d" % c, [P, M], F32) for c in range(12)]
 
-        nc.vector.memset(pk[0][:].bitcast(I32), 0)
-        nc.vector.memset(dummy[:], 0.0)
-        nc.vector.memset(pk[1][:].bitcast(I32), 0)
-        for s in range(2):
-            for k in range(1, G):
-                nc.gpsimd.memset(planes[s, k][:].bitcast(I32), 0)
-        nc.gpsimd.memset(s3[:].rearrange("p g n -> p (g n)").bitcast(I32), 0)
         nc.gpsimd.memset(b3rows[:], 0.0)
         make_identity(nc, ident[:])
+        nc.vector.memset(dummy[:], 0.0)
+        nc.vector.memset(s1[:].rearrange("p g n -> p (g n)").bitcast(I32), 0)
+        nc.gpsimd.memset(pk[:].bitcast(I32), 0)
+        for k in range(1, G):
+            nc.gpsimd.memset(planes[k][:].bitcast(I32), 0)
+        nc.gpsimd.memset(s3[:].rearrange("p g n -> p (g n)").bitcast(I32), 0)
 
         def load_theta(g):
             nc.sync.dma_start(out=th[g][:], in_=theta[512 * g : 512 * (g + 1), :].rearrange("(p j) m -> p j m", j=T))
@@ -89,39 +84,40 @@ def tile_ensemble_td_updates_t2_kernel(
                 in_=w1_words.rearrange("k p c -> p k c")[:, :, 1024 * g : 1024 * (g + 1)].bitcast(I32),
             )
 
-        def load_packed_scales(queue, s, scales):
-            for quad in range(4):
-                row = 32 * quad
-                queue.dma_start(
-                    out=pk[s][row : row + 12, :].bitcast(I32),
-                    in_=scales[:, 4 * quad : 4 * quad + 4, :].bitcast(I32),
-                )
-
-        def load_scales3():
+        def load_packed_scales():
             for quad in range(4):
                 nc.sync.dma_start(
-                    out=s3[32 * quad : 32 * quad + 4, :, :].bitcast(I32),
-                    in_=w3_scales[:, 4 * quad : 4 * quad + 4, :].rearrange("k r n -> r k n").bitcast(I32),
+                    out=pk[32 * quad : 32 * quad + 12, :].bitcast(I32),
+                    in_=w2_scales[:, 4 * quad : 4 * quad + 4, :].bitcast(I32),
                 )
 
-        def spread_scales(queue, s, k):
+        def load_planes(tile, scales):
+            for quad in range(4):
+                nc.sync.dma_start(
+                    out=tile[32 * quad : 32 * quad + 4, :, :].bitcast(I32),
+                    in_=scales[:, 4 * quad : 4 * quad + 4, :].rearrange("k r n -> r k n").bitcast(I32),
+                )
+
+        def spread_scales(k):
             for quad in range(4):
                 row = 32 * quad + 4 * k
-                queue.dma_start(
-                    out=planes[s, k][32 * quad : 32 * quad + 4, :].bitcast(I32), in_=pm[s][row : row + 4, :].bitcast(I32)
+                nc.sync.dma_start(
+                    out=planes[k][32 * quad : 32 * quad + 4, :].bitcast(I32), in_=pm[row : row + 4, :].bitcast(I32)
                 )
 
-        def load_w(raw, words, k):
-            nc.sync.dma_start(out=raw[:, k, :].bitcast(I32), in_=words[k].bitcast(I32))
-
-        load_theta(0)
-        load_packed_scales(nc.scalar, 0, w1_scales)
         nc.scalar.activation(out=dummy[:], in_=dummy[:], func=ACTF.Identity, scale=1.0)
         load_w1(0)
+        nc.sync.dma_start(out=b3rows[0:12, :], in_=b3.rearrange("(c p) -> c p", p=P))
+        load_theta(0)
+        load_planes(s1, w1_scales)
         load_theta(1)
         load_w1(1)
         load_theta(2)
+        nc.sync.dma_start(out=bsb[0][:], in_=b1.rearrange("(g p t) -> p g t", p=P, t=T))
+        nc.sync.dma_start(out=bsb[1][:], in_=b2.rearrange("(g p t) -> p g t", p=P, t=T))
         load_w1(2)
+        load_packed_scales()
+        nc.sync.dma_start(out=w2raw[:].bitcast(I32), in_=w2_words.rearrange("k p c -> p k c").bitcast(I32))
 
         def interleave(engine, dst, src, c0, c1):
             if c0 < c1:
@@ -150,9 +146,11 @@ def tile_ensemble_td_updates_t2_kernel(
 
         def perm_codes(s, g, k):
             raw = w1raw[g][:, k, :] if s == 0 else w2raw[:, k, 1024 * g : 1024 * (g + 1)]
-            eng = nc.gpsimd if (s, g, k) in ON_GPSIMD else nc.vector
+            name = "wp%d%d%d" % (s, g, k)
+            wp[s, g, k] = pool.tile([P, T, 256], U8, name=name, tag=REUSE.get((s, g, k), name), align_bytes=64)
+            eng = nc.gpsimd if (s, g, k) in REUSE else nc.vector
             eng.tensor_copy(
-                out=wp[s, g][:, k, :, :].rearrange("p t (f b) -> p t f b", b=2),
+                out=wp[s, g, k][:].rearrange("p t (f b) -> p t f b", b=2),
                 in_=raw.rearrange("p (f t b) -> p t f b", t=T, b=2),
             )
 
@@ -162,8 +160,8 @@ def tile_ensemble_td_updates_t2_kernel(
             if k == 0:
                 acc[s, g, t] = bank((4 * g + t + 4 * s) % 8, "acc%d_%d_%d" % (s, g, t))
             if s < 2:
-                lhsT = wp[s, g][:, k, t, :]
-                lsc = planes[s, k][:, 512 * g + P * t : 512 * g + P * (t + 1)]
+                lhsT = wp[s, g, k][:, t, :]
+                lsc = sp1[g][:, t, k, :] if s == 0 else planes[k][:, 512 * g + P * t : 512 * g + P * (t + 1)]
             else:
                 c = 4 * g + t
                 lhsT = w3raw[:, k, 256 * c : 256 * (c + 1)]
@@ -212,10 +210,14 @@ def tile_ensemble_td_updates_t2_kernel(
             for k in range(G):
                 mm(s, g, t, k)
 
-        def permute_scales(s):
+        def perm_scales1(g):
             nc.vector.tensor_copy(
-                out=pm[s][:].rearrange("p (g t f) -> p g t f", g=G, t=T),
-                in_=pk[s][:].rearrange("p (g f t) -> p g t f", g=G, t=T),
+                out=sp1[g][:], in_=s1[:, :, 512 * g : 512 * (g + 1)].rearrange("p k (f t) -> p t k f", t=T)
+            )
+
+        def permute_scales2():
+            nc.vector.tensor_copy(
+                out=pm[:].rearrange("p (g t f) -> p g t f", g=G, t=T), in_=pk[:].rearrange("p (g f t) -> p g t f", g=G, t=T)
             )
 
         def all_k(f, *args):
@@ -226,62 +228,50 @@ def tile_ensemble_td_updates_t2_kernel(
             for t in range(T):
                 f(*args, t)
 
-        iv_s(0, 0)
-        iv_v(0, 0)
-        permute_scales(0)
-        spread_scales(nc.scalar, 0, 1)
-        spread_scales(nc.sync, 0, 2)
-        nc.sync.dma_start(out=bsb[0][:], in_=b1.rearrange("(g p t) -> p g t", p=P, t=T))
-        nc.sync.dma_start(out=bsb[1][:], in_=b2.rearrange("(g p t) -> p g t", p=P, t=T))
-        nc.sync.dma_start(out=b3rows[0:12, :], in_=b3.rearrange("(c p) -> c p", p=P))
-        load_packed_scales(nc.sync, 1, w2_scales)
-        for k in range(G):
-            load_w(w2raw, w2_words, k)
-        quant(0, 0)
-        perm_codes(0, 0, 0)
-        mmk(0, 0, 0)
-        perm_codes(0, 1, 0)
-        mmk(0, 1, 0)
-        iv_s(0, 1)
-        iv_v(0, 1)
-        perm_codes(0, 0, 1)
-        quant(0, 1)
-        mmk(0, 0, 1)
-        perm_codes(0, 1, 1)
-        mmk(0, 1, 1)
-        iv_s(0, 2)
-        iv_v(0, 2)
-        perm_codes(0, 0, 2)
-        quant(0, 2)
-        mmk(0, 0, 2)
-        perm_codes(0, 1, 2)
-        mmk(0, 1, 2)
-        permute_scales(1)
-        for k in range(1, G):
-            spread_scales(nc.sync, 1, k)
-        load_scales3()
-        for k in range(G):
-            load_w(w3raw, w3_words, k)
-        all_t(st1, 0)
-        b3ps = psum.tile([P, P], BF16, name="b3ps", tag="bank0")
+        b3ps = psum.tile([P, P], BF16, name="b3ps", tag="bank7")
         nc.tensor.transpose(b3ps[:], b3rows[:], ident[:])
         nc.scalar.copy(out=b3col[:], in_=b3ps[:, 0:12])
-        iv_s(1, 0)
-        wp[0, 2] = pool.tile([P, G, T, 256], U8, name="wp02", tag="pk1", align_bytes=64)
+        for g in range(G):
+            iv_s(0, g)
+        all_k(perm_codes, 0, 0)
+        iv_v(0, 0)
+        perm_scales1(0)
+        quant(0, 0)
+        mmk(0, 0, 0)
+        perm_scales1(1)
+        perm_codes(0, 1, 0)
+        mmk(0, 1, 0)
+        perm_codes(0, 1, 1)
+        quant(0, 1)
+        mmk(0, 0, 1)
+        mmk(0, 1, 1)
+        perm_codes(0, 1, 2)
+        iv_v(0, 2)
+        perm_scales1(2)
+        quant(0, 2)
+        mmk(0, 0, 2)
+        mmk(0, 1, 2)
         all_k(perm_codes, 0, 2)
+        perm_codes(1, 0, 0)
+        all_t(st1, 0)
+        iv_s(1, 0)
         all_t(mmt, 0, 2)
         all_t(st1, 1)
         iv_s(1, 1)
+        permute_scales2()
+        for k in range(1, G):
+            spread_scales(k)
+        load_planes(s3, w3_scales)
+        nc.sync.dma_start(out=w3raw[:].bitcast(I32), in_=w3_words.rearrange("k p c -> p k c").bitcast(I32))
         iv_v(1, 0)
-        perm_codes(1, 0, 0)
         quant(1, 0)
+        perm_codes(1, 0, 1)
         mmk(1, 0, 0)
         all_t(st1, 2)
         iv_s(1, 2)
         perm_codes(1, 1, 0)
         mmk(1, 1, 0)
         iv_v(1, 2)
-        perm_codes(1, 0, 1)
         quant(1, 1)
         mmk(1, 0, 1)
         perm_codes(1, 1, 1)
@@ -291,10 +281,12 @@ def tile_ensemble_td_updates_t2_kernel(
         quant(1, 2)
         mmk(1, 0, 2)
         mmk(1, 1, 2)
+        perm_codes(1, 2, 0)
         all_t(st2, 0)
         iv_s(2, 0)
-        wp[1, 2] = pool.tile([P, G, T, 256], U8, name="wp12", tag="nv1g2", align_bytes=64)
-        all_k(perm_codes, 1, 2)
+        iv_v(2, 0)
+        perm_codes(1, 2, 1)
+        perm_codes(1, 2, 2)
         all_t(mmt, 1, 2)
         all_t(st2, 1)
         iv_s(2, 1)
@@ -303,6 +295,7 @@ def tile_ensemble_td_updates_t2_kernel(
         all_t(st2, 2)
         iv_s(2, 2)
         mmk(2, 1, 0)
+        iv_v(2, 1)
         quant(2, 1)
         mmk(2, 0, 1)
         mmk(2, 1, 1)

@@ -20,7 +20,7 @@ G = 3
 T = 4
 FLOPS = 3 * 2 * K * K * M
 
-IV_V = [[224, 0, 96], [0, 0, 0], [0, 0, 336]]
+IV_V = [[320, 0, 96], [0, 0, 0], [0, 0, 224]]
 REUSE = {(0, 2, 1): "thg2", (0, 2, 2): "thg1", (1, 0, 0): "thg0", (1, 0, 1): "nv1g0", (1, 2, 1): "nv1g2", (1, 2, 2): "nv1g1"}
 
 
@@ -114,10 +114,10 @@ def tile_ensemble_td_updates_t2_kernel(
         load_w1(1)
         load_theta(2)
         nc.sync.dma_start(out=bsb[0][:], in_=b1.rearrange("(g p t) -> p g t", p=P, t=T))
-        nc.sync.dma_start(out=bsb[1][:], in_=b2.rearrange("(g p t) -> p g t", p=P, t=T))
         load_w1(2)
         load_packed_scales()
         nc.sync.dma_start(out=w2raw[:].bitcast(I32), in_=w2_words.rearrange("k p c -> p k c").bitcast(I32))
+        nc.sync.dma_start(out=bsb[1][:], in_=b2.rearrange("(g p t) -> p g t", p=P, t=T))
 
         def interleave(engine, dst, src, c0, c1):
             if c0 < c1:
@@ -202,6 +202,34 @@ def tile_ensemble_td_updates_t2_kernel(
                 )
             nc.sync.dma_start(out=out[P * c : P * (c + 1), :], in_=osb[c][:])
 
+        def last_tile():
+            c = 11
+            for b in range(4):
+                cols = slice(P * b, P * (b + 1))
+                piece = psum.tile([P, P], F32, name="piece%d" % b, tag="bank%d" % (4 + b))
+                for k in range(G):
+                    codes, scales = q[2, k]
+                    nc.tensor.matmul_mx(
+                        out=piece[:],
+                        lhsT=w3raw[:, k, 256 * c : 256 * (c + 1)].bitcast(FP4X4),
+                        lhsT_scale=s3[:, k, P * c : P * (c + 1)],
+                        rhs=codes[:, cols].bitcast(FP8X4),
+                        rhs_scale=scales[:, cols],
+                        start=(k == 0),
+                        stop=(k == 2),
+                    )
+                if b % 2 == 1:
+                    nc.vector.tensor_scalar(
+                        out=osb[c][:, cols], in0=piece[:], scalar1=-1.0, scalar2=b3col[:, c : c + 1],
+                        op0=ALU.mult, op1=ALU.add,
+                    )
+                    half = slice(P * (b - 1), P * (b + 1))
+                    nc.sync.dma_start(out=out[P * c : P * (c + 1), half], in_=osb[c][:, half])
+                else:
+                    nc.scalar.activation(
+                        out=osb[c][:, cols], in_=piece[:], func=ACTF.Identity, bias=b3col[:, c : c + 1], scale=-1.0
+                    )
+
         def mmk(s, g, k):
             for t in range(T):
                 mm(s, g, t, k)
@@ -233,11 +261,13 @@ def tile_ensemble_td_updates_t2_kernel(
         nc.scalar.copy(out=b3col[:], in_=b3ps[:, 0:12])
         for g in range(G):
             iv_s(0, g)
-        all_k(perm_codes, 0, 0)
+        perm_codes(0, 0, 0)
+        perm_codes(0, 0, 1)
         iv_v(0, 0)
         perm_scales1(0)
         quant(0, 0)
         mmk(0, 0, 0)
+        perm_codes(0, 0, 2)
         perm_scales1(1)
         perm_codes(0, 1, 0)
         mmk(0, 1, 0)
@@ -290,23 +320,28 @@ def tile_ensemble_td_updates_t2_kernel(
         all_t(mmt, 1, 2)
         all_t(st2, 1)
         iv_s(2, 1)
+        st2(2, 0)
         quant(2, 0)
         mmk(2, 0, 0)
-        all_t(st2, 2)
+        st2(2, 1)
+        st2(2, 2)
+        st2(2, 3)
         iv_s(2, 2)
         mmk(2, 1, 0)
         iv_v(2, 1)
         quant(2, 1)
         mmk(2, 0, 1)
-        mmk(2, 1, 1)
         iv_v(2, 2)
         quant(2, 2)
         mmk(2, 0, 2)
         for t in range(T):
             st3(0, t, t % 2 == 1)
+        mmk(2, 1, 1)
         mmk(2, 1, 2)
         for t in range(T):
             st3(1, t, t % 2 == 1)
-        all_t(mmt, 2, 2)
-        for t in range(T):
+        for t in range(T - 1):
+            mmt(2, 2, t)
+        for t in range(T - 1):
             st3(2, t, t % 2 == 1)
+        last_tile()

from contextlib import ExitStack

import concourse.mybir as mybir
from concourse.masks import make_identity

F32 = mybir.dt.float32
BF16 = mybir.dt.bfloat16
U32 = mybir.dt.uint32
I32 = mybir.dt.int32
U8 = mybir.dt.uint8
FP8X4 = mybir.dt.float8_e4m3fn_x4
FP4X4 = mybir.dt.float4_e2m1fn_x4
ALU = mybir.AluOpType
ACTF = mybir.ActivationFunctionType

P = 128
K = 1536
M = 512
G = 3
T = 4
FLOPS = 3 * 2 * K * K * M

IV_V = [[320, 0, 96], [0, 0, 0], [0, 0, 224]]
REUSE = {(0, 2, 1): "thg2", (0, 2, 2): "thg1", (1, 0, 0): "thg0", (1, 0, 1): "nv1g0", (1, 2, 1): "nv1g2", (1, 2, 2): "nv1g1"}


def tile_ensemble_td_updates_t2_kernel(
    tc, theta, w1_words, w1_scales, w2_words, w2_scales, w3_words, w3_scales, b1, b2, b3, out
):
    nc = tc.nc
    with ExitStack() as ctx:
        pool = ctx.enter_context(tc.tile_pool(name="keep", bufs=1))
        psum = ctx.enter_context(tc.psum_pool(name="psum", bufs=1))
        ctx.enter_context(tc.manual_schedule())

        def sb(name, shape, dtype):
            return pool.tile(shape, dtype, name=name, tag=name, align_bytes=64)

        def bank(n, name):
            return psum.tile([P, M], F32, name=name, tag="bank%d" % n)

        dummy = sb("dummy", [P, 1], F32)
        th = [sb("th%d" % g, [P, T, M], BF16) for g in range(G)]
        thg = [sb("thg%d" % g, [P, M, T], BF16) for g in range(G)]
        q = {}
        for s in range(3):
            for g in range(G):
                q[s, g] = (sb("qc%d%d" % (s, g), [P, M], U32), sb("qs%d%d" % (s, g), [P, M], U8))
        w1raw = [sb("w1raw%d" % g, [P, G, 1024], U8) for g in range(G)]
        w2raw = sb("w2raw", [P, G, 3072], U8)
        w3raw = sb("w3raw", [P, G, 3072], U8)
        s3 = sb("s3", [P, G, K], U8)
        s1 = sb("s1", [P, G, K], U8)
        sp1 = [sb("sp1%d" % g, [P, T, G, P], U8) for g in range(G)]
        pk = sb("pk", [P, K], U8)
        pm = sb("pm", [P, K], U8)
        planes = [pm] + [sb("pl%d" % k, [P, K], U8) for k in range(1, G)]
        wp = {}
        bsb = [sb("b%d" % s, [P, G, T], BF16) for s in range(2)]
        b3rows = sb("b3rows", [P, P], BF16)
        b3col = sb("b3col", [P, 12], F32)
        ident = sb("ident", [P, P], BF16)
        nv1 = [sb("nv1%d" % g, [P, T, M], F32) for g in range(G)]
        nv1g = [sb("nv1g%d" % g, [P, M, T], BF16) for g in range(G)]
        v2 = [sb("v2%d" % g, [P, T, M], BF16) for g in range(G)]
        v2g = [sb("v2g%d" % g, [P, M, T], BF16) for g in range(G)]
        osb = [sb("o%d" % c, [P, M], F32) for c in range(12)]

        nc.gpsimd.memset(b3rows[:], 0.0)
        make_identity(nc, ident[:])
        nc.vector.memset(dummy[:], 0.0)
        nc.vector.memset(s1[:].rearrange("p g n -> p (g n)").bitcast(I32), 0)
        nc.gpsimd.memset(pk[:].bitcast(I32), 0)
        for k in range(1, G):
            nc.gpsimd.memset(planes[k][:].bitcast(I32), 0)
        nc.gpsimd.memset(s3[:].rearrange("p g n -> p (g n)").bitcast(I32), 0)

        def load_theta(g):
            nc.sync.dma_start(out=th[g][:], in_=theta[512 * g : 512 * (g + 1), :].rearrange("(p j) m -> p j m", j=T))

        def load_w1(g):
            nc.sync.dma_start(
                out=w1raw[g][:].bitcast(I32),
                in_=w1_words.rearrange("k p c -> p k c")[:, :, 1024 * g : 1024 * (g + 1)].bitcast(I32),
            )

        def load_packed_scales():
            for quad in range(4):
                nc.sync.dma_start(
                    out=pk[32 * quad : 32 * quad + 12, :].bitcast(I32),
                    in_=w2_scales[:, 4 * quad : 4 * quad + 4, :].bitcast(I32),
                )

        def load_planes(tile, scales):
            for quad in range(4):
                nc.sync.dma_start(
                    out=tile[32 * quad : 32 * quad + 4, :, :].bitcast(I32),
                    in_=scales[:, 4 * quad : 4 * quad + 4, :].rearrange("k r n -> r k n").bitcast(I32),
                )

        def spread_scales(k):
            for quad in range(4):
                row = 32 * quad + 4 * k
                nc.sync.dma_start(
                    out=planes[k][32 * quad : 32 * quad + 4, :].bitcast(I32), in_=pm[row : row + 4, :].bitcast(I32)
                )

        nc.scalar.activation(out=dummy[:], in_=dummy[:], func=ACTF.Identity, scale=1.0)
        load_w1(0)
        nc.sync.dma_start(out=b3rows[0:12, :], in_=b3.rearrange("(c p) -> c p", p=P))
        load_theta(0)
        load_planes(s1, w1_scales)
        load_theta(1)
        load_w1(1)
        load_theta(2)
        nc.sync.dma_start(out=bsb[0][:], in_=b1.rearrange("(g p t) -> p g t", p=P, t=T))
        load_w1(2)
        load_packed_scales()
        nc.sync.dma_start(out=w2raw[:].bitcast(I32), in_=w2_words.rearrange("k p c -> p k c").bitcast(I32))
        nc.sync.dma_start(out=bsb[1][:], in_=b2.rearrange("(g p t) -> p g t", p=P, t=T))

        def interleave(engine, dst, src, c0, c1):
            if c0 < c1:
                engine(
                    out=dst[:, c0:c1, :].rearrange("p (c i) t -> p c t i", i=4),
                    in_=src[:, :, c0:c1].rearrange("p t (c i) -> p c t i", i=4),
                )

        def tiles(s, g):
            return ((th, thg), (nv1, nv1g), (v2, v2g))[s]

        def iv_v(s, g):
            a, b = tiles(s, g)
            interleave(nc.vector.tensor_copy, b[g], a[g], 0, IV_V[s][g])

        def iv_s(s, g):
            a, b = tiles(s, g)
            interleave(nc.scalar.copy, b[g], a[g], IV_V[s][g], M)

        def quant(s, g):
            src = tiles(s, g)[1][g]
            codes, scales = q[s, g]
            nc.vector.quantize_mx(
                out=codes[:].bitcast(FP8X4), scales=scales[:], in_=src[:].rearrange("p m t -> p (m t)")
            )

        def perm_codes(s, g, k):
            raw = w1raw[g][:, k, :] if s == 0 else w2raw[:, k, 1024 * g : 1024 * (g + 1)]
            name = "wp%d%d%d" % (s, g, k)
            wp[s, g, k] = pool.tile([P, T, 256], U8, name=name, tag=REUSE.get((s, g, k), name), align_bytes=64)
            eng = nc.gpsimd if (s, g, k) in REUSE else nc.vector
            eng.tensor_copy(
                out=wp[s, g, k][:].rearrange("p t (f b) -> p t f b", b=2),
                in_=raw.rearrange("p (f t b) -> p t f b", t=T, b=2),
            )

        acc = {}

        def mm(s, g, t, k):
            if k == 0:
                acc[s, g, t] = bank((4 * g + t + 4 * s) % 8, "acc%d_%d_%d" % (s, g, t))
            if s < 2:
                lhsT = wp[s, g, k][:, t, :]
                lsc = sp1[g][:, t, k, :] if s == 0 else planes[k][:, 512 * g + P * t : 512 * g + P * (t + 1)]
            else:
                c = 4 * g + t
                lhsT = w3raw[:, k, 256 * c : 256 * (c + 1)]
                lsc = s3[:, k, P * c : P * (c + 1)]
            codes, scales = q[s, k]
            nc.tensor.matmul_mx(
                out=acc[s, g, t][:],
                lhsT=lhsT.bitcast(FP4X4),
                lhsT_scale=lsc,
                rhs=codes[:].bitcast(FP8X4),
                rhs_scale=scales[:],
                start=(k == 0),
                stop=(k == 2),
            )

        def st1(g, t):
            nc.vector.scalar_tensor_tensor(
                out=nv1[g][:, t, :], in0=acc[0, g, t][:], scalar=bsb[0][:, g, t : t + 1], in1=th[g][:, t, :],
                op0=ALU.subtract, op1=ALU.subtract,
            )

        def st2(g, t):
            nc.vector.scalar_tensor_tensor(
                out=v2[g][:, t, :], in0=acc[1, g, t][:], scalar=bsb[1][:, g, t : t + 1], in1=nv1[g][:, t, :],
                op0=ALU.add, op1=ALU.subtract,
            )

        def st3(g, t, on_vector):
            c = 4 * g + t
            if on_vector:
                nc.vector.tensor_scalar(
                    out=osb[c][:], in0=acc[2, g, t][:], scalar1=-1.0, scalar2=b3col[:, c : c + 1],
                    op0=ALU.mult, op1=ALU.add,
                )
            else:
                nc.scalar.activation(
                    out=osb[c][:], in_=acc[2, g, t][:], func=ACTF.Identity, bias=b3col[:, c : c + 1], scale=-1.0
                )
            nc.sync.dma_start(out=out[P * c : P * (c + 1), :], in_=osb[c][:])

        def last_tile():
            c = 11
            for b in range(4):
                cols = slice(P * b, P * (b + 1))
                piece = psum.tile([P, P], F32, name="piece%d" % b, tag="bank%d" % (4 + b))
                for k in range(G):
                    codes, scales = q[2, k]
                    nc.tensor.matmul_mx(
                        out=piece[:],
                        lhsT=w3raw[:, k, 256 * c : 256 * (c + 1)].bitcast(FP4X4),
                        lhsT_scale=s3[:, k, P * c : P * (c + 1)],
                        rhs=codes[:, cols].bitcast(FP8X4),
                        rhs_scale=scales[:, cols],
                        start=(k == 0),
                        stop=(k == 2),
                    )
                if b % 2 == 1:
                    nc.vector.tensor_scalar(
                        out=osb[c][:, cols], in0=piece[:], scalar1=-1.0, scalar2=b3col[:, c : c + 1],
                        op0=ALU.mult, op1=ALU.add,
                    )
                    half = slice(P * (b - 1), P * (b + 1))
                    nc.sync.dma_start(out=out[P * c : P * (c + 1), half], in_=osb[c][:, half])
                else:
                    nc.scalar.activation(
                        out=osb[c][:, cols], in_=piece[:], func=ACTF.Identity, bias=b3col[:, c : c + 1], scale=-1.0
                    )

        def mmk(s, g, k):
            for t in range(T):
                mm(s, g, t, k)

        def mmt(s, g, t):
            for k in range(G):
                mm(s, g, t, k)

        def perm_scales1(g):
            nc.vector.tensor_copy(
                out=sp1[g][:], in_=s1[:, :, 512 * g : 512 * (g + 1)].rearrange("p k (f t) -> p t k f", t=T)
            )

        def permute_scales2():
            nc.vector.tensor_copy(
                out=pm[:].rearrange("p (g t f) -> p g t f", g=G, t=T), in_=pk[:].rearrange("p (g f t) -> p g t f", g=G, t=T)
            )

        def all_k(f, *args):
            for k in range(G):
                f(*args, k)

        def all_t(f, *args):
            for t in range(T):
                f(*args, t)

        b3ps = psum.tile([P, P], BF16, name="b3ps", tag="bank7")
        nc.tensor.transpose(b3ps[:], b3rows[:], ident[:])
        nc.scalar.copy(out=b3col[:], in_=b3ps[:, 0:12])
        for g in range(G):
            iv_s(0, g)
        perm_codes(0, 0, 0)
        perm_codes(0, 0, 1)
        iv_v(0, 0)
        perm_scales1(0)
        quant(0, 0)
        mmk(0, 0, 0)
        perm_codes(0, 0, 2)
        perm_scales1(1)
        perm_codes(0, 1, 0)
        mmk(0, 1, 0)
        perm_codes(0, 1, 1)
        quant(0, 1)
        mmk(0, 0, 1)
        mmk(0, 1, 1)
        perm_codes(0, 1, 2)
        iv_v(0, 2)
        perm_scales1(2)
        quant(0, 2)
        mmk(0, 0, 2)
        mmk(0, 1, 2)
        all_k(perm_codes, 0, 2)
        perm_codes(1, 0, 0)
        all_t(st1, 0)
        iv_s(1, 0)
        all_t(mmt, 0, 2)
        all_t(st1, 1)
        iv_s(1, 1)
        permute_scales2()
        for k in range(1, G):
            spread_scales(k)
        load_planes(s3, w3_scales)
        nc.sync.dma_start(out=w3raw[:].bitcast(I32), in_=w3_words.rearrange("k p c -> p k c").bitcast(I32))
        iv_v(1, 0)
        quant(1, 0)
        perm_codes(1, 0, 1)
        mmk(1, 0, 0)
        all_t(st1, 2)
        iv_s(1, 2)
        perm_codes(1, 1, 0)
        mmk(1, 1, 0)
        iv_v(1, 2)
        quant(1, 1)
        mmk(1, 0, 1)
        perm_codes(1, 1, 1)
        mmk(1, 1, 1)
        perm_codes(1, 0, 2)
        perm_codes(1, 1, 2)
        quant(1, 2)
        mmk(1, 0, 2)
        mmk(1, 1, 2)
        perm_codes(1, 2, 0)
        all_t(st2, 0)
        iv_s(2, 0)
        iv_v(2, 0)
        perm_codes(1, 2, 1)
        perm_codes(1, 2, 2)
        all_t(mmt, 1, 2)
        all_t(st2, 1)
        iv_s(2, 1)
        st2(2, 0)
        quant(2, 0)
        mmk(2, 0, 0)
        st2(2, 1)
        st2(2, 2)
        st2(2, 3)
        iv_s(2, 2)
        mmk(2, 1, 0)
        iv_v(2, 1)
        quant(2, 1)
        mmk(2, 0, 1)
        iv_v(2, 2)
        quant(2, 2)
        mmk(2, 0, 2)
        for t in range(T):
            st3(0, t, t % 2 == 1)
        mmk(2, 1, 1)
        mmk(2, 1, 2)
        for t in range(T):
            st3(1, t, t % 2 == 1)
        for t in range(T - 1):
            mmt(2, 2, t)
        for t in range(T - 1):
            st3(2, t, t % 2 == 1)
        last_tile()
